import numpy as np
import ml_dtypes


def mxq(x, axis, fmt="e4m3"):
    dtype, down = {"e4m3": (ml_dtypes.float8_e4m3fn, 7), "e5m2": (ml_dtypes.float8_e5m2, 14)}[fmt]
    v = np.moveaxis(np.asarray(x, np.float32).astype(ml_dtypes.bfloat16).astype(np.float64), axis, -1)
    blocks = v.reshape(v.shape[:-1] + (-1, 32))
    amax = np.abs(blocks).max(-1, keepdims=True)
    byte = np.maximum(np.where(amax > 0, np.frexp(amax)[1] - 1 + 127, 0) - down, 1)
    scale = np.exp2(byte - 127.0)
    codes = (blocks / scale).astype(np.float32).astype(dtype).astype(np.float64)
    return np.moveaxis((codes * scale).reshape(v.shape), -1, axis)


WIDE = False


def mx_kscale(k):
    if not WIDE:
        return np.ones(k)
    levels = np.array([10, -10, 5, -5, 0])
    if k % 512:
        return np.exp2(np.random.permutation(np.resize(levels, k // 32))).repeat(32)
    a = np.empty((k // 512, 16))
    for p in range(k // 512):
        a[p, :8] = np.random.permutation(np.resize(levels, 8))
        for g in range(8):
            far = levels[np.abs(levels - a[p, g]) >= 10]
            a[p, g + 8] = far[np.random.randint(len(far))]
    return np.exp2(a.ravel()).repeat(32)


BF16 = ml_dtypes.bfloat16


def bf(x):
    return np.asarray(x, np.float32).astype(BF16)


def f64(x):
    return np.asarray(x).astype(np.float64)


E2M1 = np.array([0.0, 0.5, 1.0, 1.5, 2.0, 3.0, 4.0, 6.0, -0.0, -0.5, -1.0, -1.5, -2.0, -3.0, -4.0, -6.0])


def pack_weight(w, fmt):
    k, n = w.shape
    w = f64(bf(w)).reshape(k // 32, 32, n)
    amax = np.abs(w).max(1)
    if fmt == "e4m3":
        byte = np.frexp(amax)[1] - 1 + 127 - 7
    else:
        mant, ex = np.frexp(amax / 6.0)
        byte = np.where(mant > 0.5, ex, ex - 1) + 127
    byte = np.clip(np.where(amax > 0, byte, 1), 1, 254)
    scaled = (w * np.exp2(127.0 - byte)[:, None, :]).reshape(k, n).astype(np.float32)
    by_word = np.ascontiguousarray(scaled.reshape(k // 512, 128, 4, n).transpose(0, 1, 3, 2))
    if fmt == "e4m3":
        words = by_word.astype(ml_dtypes.float8_e4m3fn).view(np.uint8)
    else:
        c = by_word.astype(ml_dtypes.float4_e2m1fn).view(np.uint8) & 0xF
        words = c[..., 0::2] | (c[..., 1::2] << 4)
    return np.ascontiguousarray(words), np.ascontiguousarray(byte.astype(np.uint8).reshape(k // 512, 16, n))


def unpack_weight(words, scales, fmt):
    g, p, n, _ = words.shape
    if fmt == "e4m3":
        vals = np.ascontiguousarray(words).view(ml_dtypes.float8_e4m3fn).astype(np.float64)
    else:
        nib = np.empty((g, p, n, 4), np.uint8)
        nib[..., 0::2] = words & 0xF
        nib[..., 1::2] = words >> 4
        vals = E2M1[nib]
    vals = vals * np.repeat(np.exp2(scales.astype(np.float64) - 127.0), 8, axis=1)[..., None]
    return vals.transpose(0, 1, 3, 2).reshape(g * 512, n)
def pack4(w):
    words, scales = pack_weight(w, "e2m1")
    return words.reshape(words.shape[0], 128, -1), scales


def unpack4(words, scales):
    return unpack_weight(words.reshape(words.shape[0], 128, -1, 2), scales, "e2m1")


G, T, K, L, F = 4, 1024, 512, 1024, 512


def setup_inputs():
    s, t = mx_kscale(G * K), mx_kscale(G * T)
    surv = np.random.standard_normal((G, T, K)) * s.reshape(G, 1, K)
    ref = np.random.standard_normal((G, T, L)) * t.reshape(G, T, 1)
    steer = np.random.standard_normal((G * K, L)) / np.sqrt(K) / s[:, None]
    freq = 0.5 * np.random.random((G, 1, F))
    phase = np.random.random((G, 1, F))
    time = np.arange(T).reshape(1, T, 1)
    cosine = np.sqrt(2.0 / T) * np.cos(2.0 * np.pi * (freq * time + phase))
    steer_words, steer_scales = pack4(steer)
    doppler_words, doppler_scales = pack4(cosine.reshape(G * T, F) / t[:, None])
    return {"surv": bf(surv),
            "ref": bf(ref),
            "leak": bf(0.3 * np.random.standard_normal((G, L))),
            "steer_words": steer_words, "steer_scales": steer_scales,
            "doppler_words": doppler_words, "doppler_scales": doppler_scales}


def reference(surv, ref, leak, steer_words, steer_scales, doppler_words, doppler_scales):
    w = unpack4(steer_words, steer_scales).reshape(G, K, L)
    d = unpack4(doppler_words, doppler_scales).reshape(G, T, F)
    y = mxq(f64(surv), 2, "e4m3") @ w
    v = (y - f64(leak)[:, None, :]) * f64(ref)
    return mxq(v, 1, "e4m3").swapaxes(1, 2) @ d

@@ -1,0 +1,393 @@
+from contextlib import ExitStack
+
+import concourse.mybir as mybir
+from concourse.masks import make_identity
+
+G, T, K, L, F = 4, 1024, 512, 1024, 512
+FLOPS = 2 * G * T * K * L + 2 * G * L * T * F
+
+F32 = mybir.dt.float32
+BF16 = mybir.dt.bfloat16
+I32 = mybir.dt.int32
+U32 = mybir.dt.uint32
+U8 = mybir.dt.uint8
+FP8X4 = mybir.dt.float8_e4m3fn_x4
+FP4X4 = mybir.dt.float4_e2m1fn_x4
+ALU = mybir.AluOpType
+ACT = mybir.ActivationFunctionType
+
+P = 128
+PACK = 4
+PASS = P * PACK
+HALVES = T // PASS
+BLOCKS = L // P
+
+TURNED = [5,5,5,6]
+GPSIMD_EVERY = 0
+ORDER = "uusQxSm"
+
+RUN = 4
+S_BANKS = 4
+V_BANKS = 8 - S_BANKS
+
+
+def tile_passive_radar_ambiguity_s14_kernel(
+    tc, surv, ref, leak, steer_words, steer_scales, doppler_words, doppler_scales, out
+):
+    nc = tc.nc
+    with ExitStack() as ctx:
+        sb = ctx.enter_context(tc.tile_pool(name="sb", bufs=1))
+        ps = ctx.enter_context(tc.psum_pool(name="ps", bufs=1))
+        ctx.enter_context(tc.manual_schedule())
+
+        def tiles(name, count, shape, dtype):
+            return [sb.tile(shape, dtype, name="%s%d" % (name, i), align_bytes=64) for i in range(count)]
+
+        rings = {
+            "s_bank": [ps.tile([P, PASS], F32, name="s_bank%d" % i) for i in range(S_BANKS)],
+            "v_bank": [ps.tile([P, PASS], F32, name="v_bank%d" % i) for i in range(V_BANKS)],
+            "clean_ct": tiles("clean_ct", 4, [P, PASS], F32),
+            "clean_tc": tiles("clean_tc", 4, [P, PASS], F32),
+            "grouped": tiles("grouped", 2, [P, PASS * PACK], BF16),
+            "mixed": tiles("mixed", 6, [P, HALVES * PASS], BF16),
+            "mixed_codes": tiles("mixed_codes", 6, [P, HALVES * P], U32),
+            "mixed_scales": tiles("mixed_scales", 6, [P, HALVES * P], U8),
+            "result": tiles("result", 12, [P, F], F32),
+        }
+        taken = {name: 0 for name in rings}
+
+        def take(name):
+            tile = rings[name][taken[name] % len(rings[name])]
+            taken[name] += 1
+            return tile
+
+        ident = sb.tile([P, P], F32, name="ident")
+        w_scales = sb.tile([P, G * L], U8, name="w_scales", align_bytes=64)
+        d_scales = sb.tile([P, G * HALVES * F], U8, name="d_scales", align_bytes=64)
+        w_words = tiles("w_words", G, [P, 2 * L], U8)
+        d_words = tiles("d_words", G, [P, HALVES * 2 * F], U8)
+        surv_rows = tiles("surv_rows", G * HALVES, [P, PACK * K], BF16)
+        surv_codes = tiles("surv_codes", G * HALVES, [P, PASS], U32)
+        surv_scales = tiles("surv_scales", G * HALVES, [P, PASS], U8)
+        ref_width = [L // 2] + [L] * (G - 1)
+        ref_rows = {
+            (g, h): tiles("ref_rows%d_%d_" % (g, h), L // ref_width[g], [P, PACK * ref_width[g]], BF16)
+            for g in range(G)
+            for h in range(HALVES)
+        }
+        leak_rows = sb.tile([G * BLOCKS, P], BF16, name="leak_rows")
+        leak_neg_rows = sb.tile([P, P], F32, name="leak_neg_rows")
+        leak_neg = sb.tile([P, G * BLOCKS], F32, name="leak_neg")
+        leak_spread = tiles("leak_spread", G, [P, (BLOCKS - min(TURNED)) * P], F32)
+        warm = sb.tile([P, 1], F32, name="warm")
+
+        def load_surv(g, h):
+            nc.sync.dma_start(
+                out=surv_rows[HALVES * g + h][:].rearrange("p (t k) -> p t k", t=PACK),
+                in_=surv[g, h * PASS : (h + 1) * PASS, :].rearrange("(p t) k -> p t k", t=PACK),
+            )
+
+        def load_ref(g, h, side):
+            nc.sync.dma_start(
+                out=ref_rows[g, h][side][:].rearrange("p (t c) -> p t c", t=PACK),
+                in_=ref[g, h * PASS : (h + 1) * PASS, side * ref_width[g] : (side + 1) * ref_width[g]].rearrange(
+                    "(p t) c -> p t c", t=PACK
+                ),
+            )
+
+        def load_w(g):
+            nc.sync.dma_start(out=w_words[g][:].bitcast(I32), in_=steer_words[g].bitcast(I32))
+
+        def load_d(g):
+            nc.sync.dma_start(
+                out=d_words[g][:].bitcast(I32).rearrange("p (h n) -> p h n", h=HALVES),
+                in_=doppler_words[HALVES * g : HALVES * (g + 1)].bitcast(I32).rearrange("h p n -> p h n"),
+            )
+
+        def load_scales(plane, rows):
+            for q in range(4):
+                nc.sync.dma_start(
+                    out=plane[32 * q : 32 * q + 4, :].bitcast(I32).rearrange("r (g n) -> r g n", g=rows.shape[0]),
+                    in_=rows[:, 4 * q : 4 * q + 4, :].bitcast(I32).rearrange("g r n -> r g n"),
+                )
+
+        def turn_surv(g, h, pair, grouped, copy):
+            words = surv_rows[HALVES * g + h][:].bitcast(F32)
+            bank = take("s_bank")
+            for s in range(2):
+                t = 2 * pair + s
+                for u in range(2):
+                    nc.tensor.transpose(
+                        bank[:, (2 * s + u) * P : (2 * s + u + 1) * P],
+                        words[:, 2 * P * t + u : 2 * P * (t + 1) : 2],
+                        ident[:],
+                    )
+            copy(
+                out=grouped[:].bitcast(F32)[:, pair * PASS : (pair + 1) * PASS].rearrange(
+                    "p (s r u) -> p s r u", s=2, u=2
+                ),
+                in_=bank[:].rearrange("p (s u r) -> p s r u", s=2, u=2),
+            )
+
+        def quantise_surv(g, h, grouped):
+            nc.vector.quantize_mx(
+                out=surv_codes[HALVES * g + h][:].bitcast(FP8X4),
+                scales=surv_scales[HALVES * g + h][:],
+                in_=grouped[:],
+            )
+
+        def spread_leak(g, blocks):
+            for j0 in range(0, len(blocks), PACK):
+                bank = take("s_bank")
+                some = blocks[j0 : j0 + PACK]
+                for j, b in enumerate(some):
+                    m = BLOCKS * g + b
+                    nc.tensor.transpose(
+                        bank[:, j * P : (j + 1) * P], leak_neg[:, m : m + 1].to_broadcast([P, P]), ident[:]
+                    )
+                nc.scalar.copy(out=leak_spread[g][:, j0 * P : (j0 + len(some)) * P], in_=bank[:, : len(some) * P])
+
+        def w_block(g, b):
+            return (
+                w_words[g][:, 2 * P * b : 2 * P * (b + 1)].bitcast(FP4X4),
+                w_scales[:, g * L + P * b : g * L + P * (b + 1)],
+            )
+
+        def steer_cells_first(g, b, h):
+            words, scales = w_block(g, b)
+            bank = take("s_bank")
+            nc.tensor.matmul_mx(
+                out=bank[:],
+                lhsT=words,
+                lhsT_scale=scales,
+                rhs=surv_codes[HALVES * g + h][:].bitcast(FP8X4),
+                rhs_scale=surv_scales[HALVES * g + h][:],
+                start=True,
+                stop=True,
+            )
+            clean = take("clean_ct")
+            m = BLOCKS * g + b
+            nc.scalar.activation(out=clean[:], in_=bank[:], func=ACT.Identity, bias=leak_neg[:, m : m + 1], scale=1.0)
+            return clean
+
+        def turn_clean(clean):
+            bank = take("v_bank")
+            for t in range(PACK):
+                nc.tensor.transpose(bank[:, t * P : (t + 1) * P], clean[:, t * P : (t + 1) * P], ident[:])
+            return bank
+
+        def steer_time_first(g, b, h):
+            words, scales = w_block(g, b)
+            bank = take("v_bank")
+            for t in range(PACK):
+                nc.tensor.matmul_mx(
+                    out=bank[:, t * P : (t + 1) * P],
+                    lhsT=surv_codes[HALVES * g + h][:, t * P : (t + 1) * P].bitcast(FP8X4),
+                    lhsT_scale=surv_scales[HALVES * g + h][:, t * P : (t + 1) * P],
+                    rhs=words,
+                    rhs_scale=scales,
+                    start=True,
+                    stop=True,
+                )
+            return bank
+
+        def ref_block(g, b, h):
+            side, c0 = divmod(b * P, ref_width[g])
+            return ref_rows[g, h][side][:].rearrange("p (t c) -> p t c", t=PACK)[:, :, c0 : c0 + P]
+
+        def subtract_leak(g, j, bank, interleave):
+            clean = take("clean_tc")
+            spread = leak_spread[g][:, j * P : (j + 1) * P]
+            if interleave:
+                nc.vector.tensor_tensor(
+                    out=clean[:].rearrange("p (c t) -> p c t", t=PACK),
+                    in0=bank[:].rearrange("p (t c) -> p c t", t=PACK),
+                    in1=spread.unsqueeze(2).to_broadcast([P, P, PACK]),
+                    op=ALU.add,
+                )
+            else:
+                nc.vector.tensor_tensor(
+                    out=clean[:].rearrange("p (t c) -> p t c", t=PACK),
+                    in0=bank[:].rearrange("p (t c) -> p t c", t=PACK),
+                    in1=spread.unsqueeze(1).to_broadcast([P, PACK, P]),
+                    op=ALU.add,
+                )
+            return clean
+
+        def mix(g, b, h, clean, mixed):
+            nc.vector.tensor_tensor(
+                out=mixed[:, h * PASS : (h + 1) * PASS].rearrange("p (c i t) -> p c t i", i=RUN, t=PACK),
+                in0=clean[:].rearrange("p (t c i) -> p c t i", t=PACK, i=RUN),
+                in1=ref_block(g, b, h).rearrange("p t (c i) -> p c t i", i=RUN),
+                op=ALU.mult,
+            )
+
+        def mix_gpsimd(g, b, h, clean, mixed):
+            nc.gpsimd.tensor_tensor(
+                out=mixed[:, h * PASS : (h + 1) * PASS].rearrange("p (c t) -> p c t", t=PACK),
+                in0=clean[:].rearrange("p (c t) -> p c t", t=PACK),
+                in1=ref_block(g, b, h).rearrange("p t c -> p c t"),
+                op=ALU.mult,
+            )
+
+        def quantise_mixed(mixed):
+            codes, scales = take("mixed_codes"), take("mixed_scales")
+            nc.vector.quantize_mx(out=codes[:].bitcast(FP8X4), scales=scales[:], in_=mixed[:])
+            return codes, scales
+
+        def doppler(g, b, codes, scales, copy=nc.scalar.copy):
+            bank = take("s_bank")
+            for h in range(HALVES):
+                nc.tensor.matmul_mx(
+                    out=bank[:],
+                    lhsT=codes[:, h * P : (h + 1) * P].bitcast(FP8X4),
+                    lhsT_scale=scales[:, h * P : (h + 1) * P],
+                    rhs=d_words[g][:, h * 2 * F : (h + 1) * 2 * F].bitcast(FP4X4),
+                    rhs_scale=d_scales[:, (HALVES * g + h) * F : (HALVES * g + h + 1) * F],
+                    start=(h == 0),
+                    stop=(h == HALVES - 1),
+                )
+            result = take("result")
+            copy(out=result[:], in_=bank[:])
+            nc.sync.dma_start(out=out[g, b * P : (b + 1) * P, :], in_=result[:])
+
+        plan, direct_blocks = [], []
+        for g in range(G):
+            count = TURNED[g]
+            turned_units = [divmod(n, HALVES) for n in range(HALVES * count)]
+            direct_units = [divmod(n, HALVES) for n in range(HALVES * (BLOCKS - count))]
+            if g == 0:
+                turned_units[1:3] = turned_units[2:0:-1]
+                direct_units[1:3] = direct_units[2:0:-1]
+            number = {}
+            for i in range(count):
+                direct = direct_units[len(direct_units) * i // count : len(direct_units) * (i + 1) // count]
+                if g == 0:
+                    direct = direct_units[-(-len(direct_units) * i // count) : -(-len(direct_units) * (i + 1) // count)]
+                turned = turned_units[HALVES * i : HALVES * (i + 1)]
+                for kind, units in (("direct", direct), ("turned", turned)):
+                    for j, h in units:
+                        number.setdefault((kind, j), len(number))
+                plan.append(
+                    (g, i, [(number["turned", j], h) for j, h in turned], [(j, number["direct", j], h) for j, h in direct])
+                )
+            direct_blocks.append([number["direct", j] for j in range(BLOCKS - count)])
+
+        nc.vector.memset(w_scales[:].bitcast(I32), 0)
+        nc.gpsimd.memset(warm[:], 0.0)
+        nc.scalar.activation(out=warm[:], in_=warm[:], func=ACT.Identity, bias=0.0, scale=1.0)
+        nc.sync.dma_start(out=leak_rows[:], in_=leak.rearrange("g (b p) -> (g b) p", p=P))
+        load_surv(0, 0)
+        load_scales(w_scales, steer_scales)
+        load_surv(0, 1)
+        load_w(0)
+        make_identity(nc, ident[:])
+        nc.vector.memset(leak_neg_rows[:], 0.0)
+        nc.vector.memset(d_scales[:].bitcast(I32), 0)
+        for h in range(HALVES):
+            load_ref(0, h, 0)
+        load_surv(1, 0)
+        load_scales(d_scales, doppler_scales)
+        load_d(0)
+        load_surv(1, 1)
+        for h in range(HALVES):
+            load_ref(0, h, 1)
+        for g in range(1, G):
+            load_w(g)
+            for h in range(HALVES):
+                load_ref(g, h, 0)
+            load_d(g)
+            if g + 1 < G:
+                for h in range(HALVES):
+                    load_surv(g + 1, h)
+
+        nc.vector.tensor_scalar(
+            out=leak_neg_rows[: G * BLOCKS, :], in0=leak_rows[:], scalar1=-1.0, scalar2=None, op0=ALU.mult
+        )
+        first = [take("grouped"), take("grouped")]
+        bank = take("s_bank")
+        nc.tensor.transpose(bank[:, :P], leak_neg_rows[:], ident[:])
+        nc.scalar.copy(out=leak_neg[:], in_=bank[:, : G * BLOCKS])
+        turn_surv(0, 0, 0, first[0], nc.scalar.copy)
+        turn_surv(0, 0, 1, first[0], nc.vector.tensor_copy)
+        spread_leak(0, direct_blocks[0])
+        quantise_surv(0, 0, first[0])
+        turn_surv(0, 1, 0, first[1], nc.scalar.copy)
+        turn_surv(0, 1, 1, first[1], nc.scalar.copy)
+
+        to_quantise, to_multiply, to_mix, surv_ready = [], [], [], [(0, 1, first[1])]
+        mixed_of, halves_done = {}, {}
+        direct_count = 0
+
+        def mix_unit(how, g, b, h, clean):
+            if (g, b) not in mixed_of:
+                mixed_of[g, b] = take("mixed")
+            how(g, b, h, clean, mixed_of[g, b])
+            halves_done[g, b] = halves_done.get((g, b), 0) + 1
+            if halves_done[g, b] == HALVES:
+                to_quantise.append((g, b))
+
+        cleans = [steer_cells_first(0, b, h) for b, h in plan[0][2]]
+        for n, (g, i, turned, direct) in enumerate(plan):
+            count = TURNED[g]
+            banks = [steer_time_first(g, b, h) for j, b, h in direct]
+            ready = list(to_quantise)
+            to_quantise.clear()
+            quantised, pending = [], []
+            todo = list(zip(direct, banks))
+            for what in ORDER:
+                if what == "u" and to_mix:
+                    mix_unit(mix, *to_mix.pop(0))
+                if what in "sS":
+                    for (j, b, h), bank in todo[:1] if what == "s" else todo:
+                        direct_count += 1
+                        on = GPSIMD_EVERY and direct_count % GPSIMD_EVERY == 1 % GPSIMD_EVERY
+                        clean = subtract_leak(g, j, bank, on)
+                        if on:
+                            mix_unit(mix_gpsimd, g, b, h, clean)
+                        else:
+                            pending.append((g, b, h, clean))
+                    todo = todo[1:] if what == "s" else []
+                if what == "q":
+                    for gq, b in ready:
+                        quantised.append((gq, b) + quantise_mixed(mixed_of[gq, b]))
+                if what == "Q":
+                    for gq, b in ready + to_quantise:
+                        quantised.append((gq, b) + quantise_mixed(mixed_of[gq, b]))
+                    to_quantise.clear()
+                if what == "m":
+                    for args in pending:
+                        mix_unit(mix, *args)
+                if what == "x":
+                    for args in surv_ready:
+                        quantise_surv(*args)
+                    surv_ready = []
+            for args in to_multiply:
+                doppler(*args)
+            to_multiply = quantised
+            if n + 1 < len(plan):
+                cleans_next = [steer_cells_first(plan[n + 1][0], b, h) for b, h in plan[n + 1][2]]
+
+            to_mix = [(g, b, h, turn_clean(clean)) for (b, h), clean in zip(turned, cleans)]
+            cleans = cleans_next
+            if g + 1 < G:
+                for c in range(2 * HALVES):
+                    if c * (count - 2) // 4 == i:
+                        h, pair = divmod(c, 2)
+                        if pair == 0:
+                            grouped = take("grouped")
+                        turn_surv(g + 1, h, pair, grouped, nc.scalar.copy)
+                        if pair == 1:
+                            surv_ready.append((g + 1, h, grouped))
+                if i == count - 1:
+                    spread_leak(g + 1, direct_blocks[g + 1])
+
+        ready = list(to_quantise)
+        to_quantise.clear()
+        mix_unit(mix, *to_mix[0])
+        quantised = [(gq, b) + quantise_mixed(mixed_of[gq, b]) for gq, b in ready]
+        mix_unit(mix, *to_mix[1])
+        for args in to_multiply + quantised:
+            doppler(*args)
+        for gq, b in to_quantise:
+            doppler(gq, b, *quantise_mixed(mixed_of[gq, b]), copy=nc.vector.tensor_copy)

@@ -22,11 +22,13 @@ PASS = P * PACK
 HALVES = T // PASS
 BLOCKS = L // P
 
-TURNED = [5,5,5,6]
-GPSIMD_EVERY = 0
-ORDER = "uusQxSm"
+TURNED = [4,4,4,4]
+GPSIMD_EVERY = 2
+ORDER = "xOYASTuuqmC"
 
 RUN = 4
+LAG = 2
+SORT = "D" in ORDER
 S_BANKS = 4
 V_BANKS = 8 - S_BANKS
 
@@ -48,10 +50,11 @@ def tile_passive_radar_ambiguity_s14_kernel(
             "v_bank": [ps.tile([P, PASS], F32, name="v_bank%d" % i) for i in range(V_BANKS)],
             "clean_ct": tiles("clean_ct", 4, [P, PASS], F32),
             "clean_tc": tiles("clean_tc", 4, [P, PASS], F32),
+            "sorted": tiles("sorted", 4, [P, PASS], F32),
             "grouped": tiles("grouped", 2, [P, PASS * PACK], BF16),
             "mixed": tiles("mixed", 6, [P, HALVES * PASS], BF16),
-            "mixed_codes": tiles("mixed_codes", 6, [P, HALVES * P], U32),
-            "mixed_scales": tiles("mixed_scales", 6, [P, HALVES * P], U8),
+            "mixed_codes": tiles("mixed_codes", 8, [P, HALVES * P], U32),
+            "mixed_scales": tiles("mixed_scales", 8, [P, HALVES * P], U8),
             "result": tiles("result", 12, [P, F], F32),
         }
         taken = {name: 0 for name in rings}
@@ -111,15 +114,29 @@ def tile_passive_radar_ambiguity_s14_kernel(
                     in_=rows[:, 4 * q : 4 * q + 4, :].bitcast(I32).rearrange("g r n -> r g n"),
                 )
 
+        sorted_of = {}
+
+        def sort_words(g, h, pair, copy=nc.scalar.copy):
+            tile = take("sorted")
+            words = surv_rows[HALVES * g + h][:].bitcast(F32)[:, pair * PASS : (pair + 1) * PASS]
+            copy(
+                out=tile[:].rearrange("p (s u r) -> p s u r", s=2, u=2),
+                in_=words.rearrange("p (s r u) -> p s u r", s=2, u=2),
+            )
+            sorted_of[g, h, pair] = tile
+
         def turn_surv(g, h, pair, grouped, copy):
             words = surv_rows[HALVES * g + h][:].bitcast(F32)
             bank = take("s_bank")
+            presorted = sorted_of.get((g, h, pair))
             for s in range(2):
                 t = 2 * pair + s
                 for u in range(2):
                     nc.tensor.transpose(
                         bank[:, (2 * s + u) * P : (2 * s + u + 1) * P],
-                        words[:, 2 * P * t + u : 2 * P * (t + 1) : 2],
+                        words[:, 2 * P * t + u : 2 * P * (t + 1) : 2]
+                        if presorted is None
+                        else presorted[:, (2 * s + u) * P : (2 * s + u + 1) * P],
                         ident[:],
                     )
             copy(
@@ -256,13 +273,15 @@ def tile_passive_radar_ambiguity_s14_kernel(
             count = TURNED[g]
             turned_units = [divmod(n, HALVES) for n in range(HALVES * count)]
             direct_units = [divmod(n, HALVES) for n in range(HALVES * (BLOCKS - count))]
-            if g == 0:
+            if g == 0 or 1:
                 turned_units[1:3] = turned_units[2:0:-1]
                 direct_units[1:3] = direct_units[2:0:-1]
             number = {}
             for i in range(count):
                 direct = direct_units[len(direct_units) * i // count : len(direct_units) * (i + 1) // count]
-                if g == 0:
+                if g == G - 1 and 0:
+                    direct = direct_units[-(-len(direct_units) * i // (count - 1)) : -(-len(direct_units) * (i + 1) // (count - 1))]
+                elif g == 0 or 1:
                     direct = direct_units[-(-len(direct_units) * i // count) : -(-len(direct_units) * (i + 1) // count)]
                 turned = turned_units[HALVES * i : HALVES * (i + 1)]
                 for kind, units in (("direct", direct), ("turned", turned)):
@@ -273,25 +292,39 @@ def tile_passive_radar_ambiguity_s14_kernel(
                 )
             direct_blocks.append([number["direct", j] for j in range(BLOCKS - count)])
 
+        make_identity(nc, ident[:])
         nc.vector.memset(w_scales[:].bitcast(I32), 0)
         nc.gpsimd.memset(warm[:], 0.0)
         nc.scalar.activation(out=warm[:], in_=warm[:], func=ACT.Identity, bias=0.0, scale=1.0)
         nc.sync.dma_start(out=leak_rows[:], in_=leak.rearrange("g (b p) -> (g b) p", p=P))
-        load_surv(0, 0)
-        load_scales(w_scales, steer_scales)
+        for pair in range(2):
+            nc.sync.dma_start(
+                out=surv_rows[0][:, pair * 2 * K : (pair + 1) * 2 * K].rearrange("p (t k) -> p t k", t=2),
+                in_=surv[0, :PASS, :].rearrange("(p t) k -> p t k", t=PACK)[:, 2 * pair : 2 * pair + 2, :],
+            )
         load_surv(0, 1)
+        load_scales(w_scales, steer_scales)
         load_w(0)
-        make_identity(nc, ident[:])
         nc.vector.memset(leak_neg_rows[:], 0.0)
         nc.vector.memset(d_scales[:].bitcast(I32), 0)
-        for h in range(HALVES):
-            load_ref(0, h, 0)
-        load_surv(1, 0)
-        load_scales(d_scales, doppler_scales)
-        load_d(0)
-        load_surv(1, 1)
-        for h in range(HALVES):
-            load_ref(0, h, 1)
+        for what in "rRad0b1":
+            if what == "r":
+                load_ref(0, 0, 0)
+            if what == "s":
+                load_surv(0, 1)
+            if what == "R":
+                load_ref(0, 1, 0)
+            if what == "a":
+                load_surv(1, 0)
+            if what == "b":
+                load_surv(1, 1)
+            if what == "d":
+                load_scales(d_scales, doppler_scales)
+                load_d(0)
+            if what == "0":
+                load_ref(0, 0, 1)
+            if what == "1":
+                load_ref(0, 1, 1)
         for g in range(1, G):
             load_w(g)
             for h in range(HALVES):
@@ -305,10 +338,16 @@ def tile_passive_radar_ambiguity_s14_kernel(
             out=leak_neg_rows[: G * BLOCKS, :], in0=leak_rows[:], scalar1=-1.0, scalar2=None, op0=ALU.mult
         )
         first = [take("grouped"), take("grouped")]
+        if 1:
+            sort_words(0, 0, 0, nc.vector.tensor_copy)
+            sort_words(0, 0, 1, nc.vector.tensor_copy)
         bank = take("s_bank")
         nc.tensor.transpose(bank[:, :P], leak_neg_rows[:], ident[:])
         nc.scalar.copy(out=leak_neg[:], in_=bank[:, : G * BLOCKS])
         turn_surv(0, 0, 0, first[0], nc.scalar.copy)
+        if 1:
+            sort_words(0, 1, 0, nc.vector.tensor_copy)
+            sort_words(0, 1, 1, nc.vector.tensor_copy)
         turn_surv(0, 0, 1, first[0], nc.vector.tensor_copy)
         spread_leak(0, direct_blocks[0])
         quantise_surv(0, 0, first[0])
@@ -318,6 +357,7 @@ def tile_passive_radar_ambiguity_s14_kernel(
         to_quantise, to_multiply, to_mix, surv_ready = [], [], [], [(0, 1, first[1])]
         mixed_of, halves_done = {}, {}
         direct_count = 0
+        surv_next = []
 
         def mix_unit(how, g, b, h, clean):
             if (g, b) not in mixed_of:
@@ -327,21 +367,56 @@ def tile_passive_radar_ambiguity_s14_kernel(
             if halves_done[g, b] == HALVES:
                 to_quantise.append((g, b))
 
-        cleans = [steer_cells_first(0, b, h) for b, h in plan[0][2]]
+        to_multiply = [[] for lag in range(LAG)]
+        pending = []
         for n, (g, i, turned, direct) in enumerate(plan):
             count = TURNED[g]
-            banks = [steer_time_first(g, b, h) for j, b, h in direct]
             ready = list(to_quantise)
             to_quantise.clear()
-            quantised, pending = [], []
-            todo = list(zip(direct, banks))
-            for what in ORDER:
+            quantised = []
+            for what in ("xAySYmTuuOC" if n == 0 else "xOYASTuuqmC" if n == len(plan) - 1 else ORDER):
+                if what == "y":
+                    cleans = [steer_cells_first(g, b, h) for b, h in turned]
+                if what == "p":
+                    sort_words(0, 1, 0)
+                    sort_words(0, 1, 1)
+                if what == "P":
+                    turn_surv(0, 1, 0, first[1], nc.scalar.copy)
+                    turn_surv(0, 1, 1, first[1], nc.scalar.copy)
+                    surv_ready.append((0, 1, first[1]))
+                if what == "A":
+                    todo = [(unit, steer_time_first(g, unit[1], unit[2])) for unit in direct]
+                if what == "O":
+                    for args in to_multiply.pop(0):
+                        doppler(*args)
+                if what == "Y" and n + 1 < len(plan):
+                    cleans_next = [steer_cells_first(plan[n + 1][0], b, h) for b, h in plan[n + 1][2]]
+                if what == "T":
+                    to_mix.extend([(g, b, h, turn_clean(clean)) for (b, h), clean in zip(turned, cleans)])
+                if what == "C" and g + 1 < G:
+                    for c in range(2 * HALVES):
+                        if min(c, count - 2) == i:
+                            h, pair = divmod(c, 2)
+                            if pair == 0:
+                                grouped = take("grouped")
+                            turn_surv(g + 1, h, pair, grouped, nc.scalar.copy)
+                            if pair == 1:
+                                surv_next.append((g + 1, h, grouped))
+                    if i == count - 1:
+                        spread_leak(g + 1, direct_blocks[g + 1])
+                if what == "D" and g + 1 < G:
+                    for c in range(2 * HALVES):
+                        if (min(c, count - 2) == i + 1 and (g or i + 1 > min([min(c, count - 2) for c in range(4)]))) or (g == 0 and i == min(c, count - 2) == (min(c, count - 2) if c == 0 else i) and i == min([min(c, count - 2) for c in range(4)])):
+                            sort_words(g + 1, *divmod(c, 2))
+                        if i == count - 1 and g + 2 < G and c * (count - 2) // 4 == 0:
+                            sort_words(g + 2, *divmod(c, 2))
                 if what == "u" and to_mix:
                     mix_unit(mix, *to_mix.pop(0))
                 if what in "sS":
                     for (j, b, h), bank in todo[:1] if what == "s" else todo:
                         direct_count += 1
-                        on = GPSIMD_EVERY and direct_count % GPSIMD_EVERY == 1 % GPSIMD_EVERY
+                        first_here = (j, b, h) == direct[0]
+                        on = first_here
                         clean = subtract_leak(g, j, bank, on)
                         if on:
                             mix_unit(mix_gpsimd, g, b, h, clean)
@@ -358,36 +433,22 @@ def tile_passive_radar_ambiguity_s14_kernel(
                 if what == "m":
                     for args in pending:
                         mix_unit(mix, *args)
+                    pending = []
                 if what == "x":
                     for args in surv_ready:
                         quantise_surv(*args)
                     surv_ready = []
-            for args in to_multiply:
-                doppler(*args)
-            to_multiply = quantised
-            if n + 1 < len(plan):
-                cleans_next = [steer_cells_first(plan[n + 1][0], b, h) for b, h in plan[n + 1][2]]
-
-            to_mix = [(g, b, h, turn_clean(clean)) for (b, h), clean in zip(turned, cleans)]
+            to_multiply.append(quantised)
             cleans = cleans_next
-            if g + 1 < G:
-                for c in range(2 * HALVES):
-                    if c * (count - 2) // 4 == i:
-                        h, pair = divmod(c, 2)
-                        if pair == 0:
-                            grouped = take("grouped")
-                        turn_surv(g + 1, h, pair, grouped, nc.scalar.copy)
-                        if pair == 1:
-                            surv_ready.append((g + 1, h, grouped))
-                if i == count - 1:
-                    spread_leak(g + 1, direct_blocks[g + 1])
+            surv_ready, surv_next = surv_ready + surv_next, []
 
-        ready = list(to_quantise)
-        to_quantise.clear()
-        mix_unit(mix, *to_mix[0])
-        quantised = [(gq, b) + quantise_mixed(mixed_of[gq, b]) for gq, b in ready]
-        mix_unit(mix, *to_mix[1])
-        for args in to_multiply + quantised:
-            doppler(*args)
-        for gq, b in to_quantise:
-            doppler(gq, b, *quantise_mixed(mixed_of[gq, b]), copy=nc.vector.tensor_copy)
+        for args in pending:
+            mix_unit(mix, *args)
+        for args in to_mix:
+            mix_unit(mix, *args)
+        for some in to_multiply:
+            for args in some:
+                doppler(*args)
+        for k, (gq, b) in enumerate(to_quantise):
+            last = k == len(to_quantise) - 1
+            doppler(gq, b, *quantise_mixed(mixed_of[gq, b]), copy=nc.vector.tensor_copy if last else nc.scalar.copy)

@@ -22,9 +22,9 @@ PASS = P * PACK
 HALVES = T // PASS
 BLOCKS = L // P
 
-TURNED = [4,4,4,4]
+SETS = [[(2,2),(3,1)],[(2,2),(3,1)],[(2,2),(3,1)],[(3,1),(3,1)]]
 GPSIMD_EVERY = 2
-ORDER = "xOYASTuuqmC"
+ORDER = "xOYASTUqmC"
 
 RUN = 4
 LAG = 2
@@ -48,14 +48,14 @@ def tile_passive_radar_ambiguity_s14_kernel(
         rings = {
             "s_bank": [ps.tile([P, PASS], F32, name="s_bank%d" % i) for i in range(S_BANKS)],
             "v_bank": [ps.tile([P, PASS], F32, name="v_bank%d" % i) for i in range(V_BANKS)],
-            "clean_ct": tiles("clean_ct", 4, [P, PASS], F32),
-            "clean_tc": tiles("clean_tc", 4, [P, PASS], F32),
-            "sorted": tiles("sorted", 4, [P, PASS], F32),
+            "clean_ct": tiles("clean_ct", 8, [P, PASS], F32),
+            "clean_tc": tiles("clean_tc", 3, [P, PASS], F32),
+            "sorted": tiles("sorted", 3, [P, PASS], F32),
             "grouped": tiles("grouped", 2, [P, PASS * PACK], BF16),
-            "mixed": tiles("mixed", 6, [P, HALVES * PASS], BF16),
+            "mixed": tiles("mixed", 8, [P, HALVES * PASS], BF16),
             "mixed_codes": tiles("mixed_codes", 8, [P, HALVES * P], U32),
             "mixed_scales": tiles("mixed_scales", 8, [P, HALVES * P], U8),
-            "result": tiles("result", 12, [P, F], F32),
+            "result": tiles("result", 10, [P, F], F32),
         }
         taken = {name: 0 for name in rings}
 
@@ -81,7 +81,7 @@ def tile_passive_radar_ambiguity_s14_kernel(
         leak_rows = sb.tile([G * BLOCKS, P], BF16, name="leak_rows")
         leak_neg_rows = sb.tile([P, P], F32, name="leak_neg_rows")
         leak_neg = sb.tile([P, G * BLOCKS], F32, name="leak_neg")
-        leak_spread = tiles("leak_spread", G, [P, (BLOCKS - min(TURNED)) * P], F32)
+        leak_spread = tiles("leak_spread", G, [P, PACK * P], F32)
         warm = sb.tile([P, 1], F32, name="warm")
 
         def load_surv(g, h):
@@ -270,27 +270,19 @@ def tile_passive_radar_ambiguity_s14_kernel(
 
         plan, direct_blocks = [], []
         for g in range(G):
-            count = TURNED[g]
-            turned_units = [divmod(n, HALVES) for n in range(HALVES * count)]
-            direct_units = [divmod(n, HALVES) for n in range(HALVES * (BLOCKS - count))]
-            if g == 0 or 1:
-                turned_units[1:3] = turned_units[2:0:-1]
-                direct_units[1:3] = direct_units[2:0:-1]
-            number = {}
-            for i in range(count):
-                direct = direct_units[len(direct_units) * i // count : len(direct_units) * (i + 1) // count]
-                if g == G - 1 and 0:
-                    direct = direct_units[-(-len(direct_units) * i // (count - 1)) : -(-len(direct_units) * (i + 1) // (count - 1))]
-                elif g == 0 or 1:
-                    direct = direct_units[-(-len(direct_units) * i // count) : -(-len(direct_units) * (i + 1) // count)]
-                turned = turned_units[HALVES * i : HALVES * (i + 1)]
-                for kind, units in (("direct", direct), ("turned", turned)):
-                    for j, h in units:
-                        number.setdefault((kind, j), len(number))
-                plan.append(
-                    (g, i, [(number["turned", j], h) for j, h in turned], [(j, number["direct", j], h) for j, h in direct])
-                )
-            direct_blocks.append([number["direct", j] for j in range(BLOCKS - count)])
+            first_block, direct_all = 0, []
+            for r, (n_turned, n_direct) in enumerate(SETS[g]):
+                blocks = list(range(first_block, first_block + n_turned + n_direct))
+                first_block += len(blocks)
+                tu = [(b, h) for b in blocks[n_direct:] for h in range(HALVES)]
+                du = [(len(direct_all) + j, b, h) for j, b in enumerate(blocks[:n_direct]) for h in range(HALVES)]
+                for h in range(HALVES):
+                    if r > 0:
+                        plan.append((g, HALVES * r + h, tu[h * n_turned : (h + 1) * n_turned], du[h * n_direct : (h + 1) * n_direct]))
+                    else:
+                        plan.append((g, HALVES * r + h, tu[h::HALVES], du[h::HALVES]))
+                direct_all.extend(blocks[:n_direct])
+            direct_blocks.append(direct_all)
 
         make_identity(nc, ident[:])
         nc.vector.memset(w_scales[:].bitcast(I32), 0)
@@ -307,7 +299,7 @@ def tile_passive_radar_ambiguity_s14_kernel(
         load_w(0)
         nc.vector.memset(leak_neg_rows[:], 0.0)
         nc.vector.memset(d_scales[:].bitcast(I32), 0)
-        for what in "rRad0b1":
+        for what in "rRab01d":
             if what == "r":
                 load_ref(0, 0, 0)
             if what == "s":
@@ -370,11 +362,12 @@ def tile_passive_radar_ambiguity_s14_kernel(
         to_multiply = [[] for lag in range(LAG)]
         pending = []
         for n, (g, i, turned, direct) in enumerate(plan):
-            count = TURNED[g]
-            ready = list(to_quantise)
-            to_quantise.clear()
+            count = HALVES * len(SETS[g])
+            share = -(-BLOCKS // count) if n < len(plan) - 1 else BLOCKS
+            ready = to_quantise[:share]
+            to_quantise[:share] = []
             quantised = []
-            for what in ("xAySYmTuuOC" if n == 0 else "xOYASTuuqmC" if n == len(plan) - 1 else ORDER):
+            for what in ("xAySYmTUOC" if n == 0 else "OASTqumoQuQouQo" if n == len(plan) - 1 else "xOYASTUqmC" if n == len(plan) - 2 else ORDER):
                 if what == "y":
                     cleans = [steer_cells_first(g, b, h) for b, h in turned]
                 if what == "p":
@@ -408,15 +401,19 @@ def tile_passive_radar_ambiguity_s14_kernel(
                     for c in range(2 * HALVES):
                         if (min(c, count - 2) == i + 1 and (g or i + 1 > min([min(c, count - 2) for c in range(4)]))) or (g == 0 and i == min(c, count - 2) == (min(c, count - 2) if c == 0 else i) and i == min([min(c, count - 2) for c in range(4)])):
                             sort_words(g + 1, *divmod(c, 2))
-                        if i == count - 1 and g + 2 < G and c * (count - 2) // 4 == 0:
+                        if i == count - 1 and g + 2 < G and c == 0:
                             sort_words(g + 2, *divmod(c, 2))
                 if what == "u" and to_mix:
                     mix_unit(mix, *to_mix.pop(0))
+                if what == "U":
+                    for args in to_mix:
+                        mix_unit(mix, *args)
+                    to_mix = []
                 if what in "sS":
                     for (j, b, h), bank in todo[:1] if what == "s" else todo:
                         direct_count += 1
                         first_here = (j, b, h) == direct[0]
-                        on = first_here
+                        on = False
                         clean = subtract_leak(g, j, bank, on)
                         if on:
                             mix_unit(mix_gpsimd, g, b, h, clean)
@@ -426,10 +423,20 @@ def tile_passive_radar_ambiguity_s14_kernel(
                 if what == "q":
                     for gq, b in ready:
                         quantised.append((gq, b) + quantise_mixed(mixed_of[gq, b]))
+                    ready = []
                 if what == "Q":
                     for gq, b in ready + to_quantise:
                         quantised.append((gq, b) + quantise_mixed(mixed_of[gq, b]))
                     to_quantise.clear()
+                    ready = []
+                if what == "o":
+                    for some in to_multiply:
+                        for args in some:
+                            doppler(*args)
+                        some.clear()
+                    for args in quantised:
+                        doppler(*args, copy=nc.vector.tensor_copy if len(halves_done) == G * BLOCKS and all([v == 2 for v in halves_done.values()]) and args is quantised[-1] and not to_quantise else nc.scalar.copy)
+                    quantised = []
                 if what == "m":
                     for args in pending:
                         mix_unit(mix, *args)

@@ -26,7 +26,7 @@ SETS = [[(2,2),(3,1)],[(2,2),(3,1)],[(2,2),(3,1)],[(3,1),(3,1)]]
 GPSIMD_EVERY = 2
 ORDER = "xOYASTUqmC"
 
-RUN = 4
+RUN = 2
 LAG = 2
 SORT = "D" in ORDER
 S_BANKS = 4
@@ -317,7 +317,7 @@ def tile_passive_radar_ambiguity_s14_kernel(
                 load_ref(0, 0, 1)
             if what == "1":
                 load_ref(0, 1, 1)
-        for g in range(1, G):
+        def load_group(g):
             load_w(g)
             for h in range(HALVES):
                 load_ref(g, h, 0)
@@ -325,6 +325,11 @@ def tile_passive_radar_ambiguity_s14_kernel(
             if g + 1 < G:
                 for h in range(HALVES):
                     load_surv(g + 1, h)
+
+        load_at = [0,-1,-1,-1]
+        for g in range(1, G):
+            if load_at[g] < 0:
+                load_group(g)
 
         nc.vector.tensor_scalar(
             out=leak_neg_rows[: G * BLOCKS, :], in0=leak_rows[:], scalar1=-1.0, scalar2=None, op0=ALU.mult
@@ -367,6 +372,9 @@ def tile_passive_radar_ambiguity_s14_kernel(
             ready = to_quantise[:share]
             to_quantise[:share] = []
             quantised = []
+            for g_load in range(1, G):
+                if load_at[g_load] == n:
+                    load_group(g_load)
             for what in ("xAySYmTUOC" if n == 0 else "OASTqumoQuQouQo" if n == len(plan) - 1 else "xOYASTUqmC" if n == len(plan) - 2 else ORDER):
                 if what == "y":
                     cleans = [steer_cells_first(g, b, h) for b, h in turned]

@@ -21,16 +21,14 @@ PACK = 4
 PASS = P * PACK
 HALVES = T // PASS
 BLOCKS = L // P
+QUAD = 4
+STEPS = HALVES * BLOCKS // QUAD
+PAIRS = 2
 
-SETS = [[(2,2),(3,1)],[(2,2),(3,1)],[(2,2),(3,1)],[(3,1),(3,1)]]
-GPSIMD_EVERY = 2
-ORDER = "xOYASTUqmC"
-
+DIRECT_IN_QUAD = ((2, 1), (1, 1))
 RUN = 2
-LAG = 2
-SORT = "D" in ORDER
-S_BANKS = 4
-V_BANKS = 8 - S_BANKS
+DOPPLER_LAG = 2
+BLOCKS_PER_STEP = BLOCKS // STEPS
 
 
 def tile_passive_radar_ambiguity_s14_kernel(
@@ -46,16 +44,16 @@ def tile_passive_radar_ambiguity_s14_kernel(
             return [sb.tile(shape, dtype, name="%s%d" % (name, i), align_bytes=64) for i in range(count)]
 
         rings = {
-            "s_bank": [ps.tile([P, PASS], F32, name="s_bank%d" % i) for i in range(S_BANKS)],
-            "v_bank": [ps.tile([P, PASS], F32, name="v_bank%d" % i) for i in range(V_BANKS)],
-            "clean_ct": tiles("clean_ct", 8, [P, PASS], F32),
-            "clean_tc": tiles("clean_tc", 3, [P, PASS], F32),
-            "sorted": tiles("sorted", 3, [P, PASS], F32),
-            "grouped": tiles("grouped", 2, [P, PASS * PACK], BF16),
-            "mixed": tiles("mixed", 8, [P, HALVES * PASS], BF16),
-            "mixed_codes": tiles("mixed_codes", 8, [P, HALVES * P], U32),
-            "mixed_scales": tiles("mixed_scales", 8, [P, HALVES * P], U8),
-            "result": tiles("result", 10, [P, F], F32),
+            "s_bank": [ps.tile([P, PASS], F32, name="s_bank%d" % i) for i in range(4)],
+            "v_bank": [ps.tile([P, PASS], F32, name="v_bank%d" % i) for i in range(4)],
+            "clean_turned": tiles("clean_turned", 6, [P, PASS], F32),
+            "clean_direct": tiles("clean_direct", 3, [P, PASS], F32),
+            "sorted_words": tiles("sorted_words", 3, [P, PASS], F32),
+            "surv_turned": tiles("surv_turned", 2, [P, PASS * PACK], BF16),
+            "mixed": tiles("mixed", 2 * QUAD, [P, HALVES * PASS], BF16),
+            "mixed_codes": tiles("mixed_codes", 2 * QUAD, [P, HALVES * P], U32),
+            "mixed_scales": tiles("mixed_scales", 2 * QUAD, [P, HALVES * P], U8),
+            "result": tiles("result", 12, [P, F], F32),
         }
         taken = {name: 0 for name in rings}
 
@@ -72,7 +70,7 @@ def tile_passive_radar_ambiguity_s14_kernel(
         surv_rows = tiles("surv_rows", G * HALVES, [P, PACK * K], BF16)
         surv_codes = tiles("surv_codes", G * HALVES, [P, PASS], U32)
         surv_scales = tiles("surv_scales", G * HALVES, [P, PASS], U8)
-        ref_width = [L // 2] + [L] * (G - 1)
+        ref_width = [QUAD * P] + [L] * (G - 1)
         ref_rows = {
             (g, h): tiles("ref_rows%d_%d_" % (g, h), L // ref_width[g], [P, PACK * ref_width[g]], BF16)
             for g in range(G)
@@ -81,21 +79,19 @@ def tile_passive_radar_ambiguity_s14_kernel(
         leak_rows = sb.tile([G * BLOCKS, P], BF16, name="leak_rows")
         leak_neg_rows = sb.tile([P, P], F32, name="leak_neg_rows")
         leak_neg = sb.tile([P, G * BLOCKS], F32, name="leak_neg")
-        leak_spread = tiles("leak_spread", G, [P, PACK * P], F32)
-        warm = sb.tile([P, 1], F32, name="warm")
+        leak_spread = tiles("leak_spread", G, [P, QUAD * P], F32)
 
-        def load_surv(g, h):
+        def load_surv(g, h, slots=slice(0, PACK)):
             nc.sync.dma_start(
-                out=surv_rows[HALVES * g + h][:].rearrange("p (t k) -> p t k", t=PACK),
-                in_=surv[g, h * PASS : (h + 1) * PASS, :].rearrange("(p t) k -> p t k", t=PACK),
+                out=surv_rows[HALVES * g + h][:, slots.start * K : slots.stop * K].rearrange("p (t k) -> p t k", k=K),
+                in_=surv[g, h * PASS : (h + 1) * PASS, :].rearrange("(p t) k -> p t k", t=PACK)[:, slots, :],
             )
 
-        def load_ref(g, h, side):
+        def load_ref(g, h, part):
+            cells = slice(part * ref_width[g], (part + 1) * ref_width[g])
             nc.sync.dma_start(
-                out=ref_rows[g, h][side][:].rearrange("p (t c) -> p t c", t=PACK),
-                in_=ref[g, h * PASS : (h + 1) * PASS, side * ref_width[g] : (side + 1) * ref_width[g]].rearrange(
-                    "(p t) c -> p t c", t=PACK
-                ),
+                out=ref_rows[g, h][part][:].rearrange("p (t c) -> p t c", t=PACK),
+                in_=ref[g, h * PASS : (h + 1) * PASS, cells].rearrange("(p t) c -> p t c", t=PACK),
             )
 
         def load_w(g):
@@ -107,62 +103,53 @@ def tile_passive_radar_ambiguity_s14_kernel(
                 in_=doppler_words[HALVES * g : HALVES * (g + 1)].bitcast(I32).rearrange("h p n -> p h n"),
             )
 
-        def load_scales(plane, rows):
+        def load_scales(scales, rows):
             for q in range(4):
                 nc.sync.dma_start(
-                    out=plane[32 * q : 32 * q + 4, :].bitcast(I32).rearrange("r (g n) -> r g n", g=rows.shape[0]),
+                    out=scales[32 * q : 32 * q + 4, :].bitcast(I32).rearrange("r (g n) -> r g n", g=rows.shape[0]),
                     in_=rows[:, 4 * q : 4 * q + 4, :].bitcast(I32).rearrange("g r n -> r g n"),
                 )
 
-        sorted_of = {}
-
-        def sort_words(g, h, pair, copy=nc.scalar.copy):
-            tile = take("sorted")
+        def sort_words(g, h, pair):
+            tile = take("sorted_words")
             words = surv_rows[HALVES * g + h][:].bitcast(F32)[:, pair * PASS : (pair + 1) * PASS]
-            copy(
+            nc.vector.tensor_copy(
                 out=tile[:].rearrange("p (s u r) -> p s u r", s=2, u=2),
                 in_=words.rearrange("p (s r u) -> p s u r", s=2, u=2),
             )
-            sorted_of[g, h, pair] = tile
+            return [tile[:, n * P : (n + 1) * P] for n in range(4)]
 
-        def turn_surv(g, h, pair, grouped, copy):
+        def stepped_words(g, h, pair):
             words = surv_rows[HALVES * g + h][:].bitcast(F32)
+            return [words[:, 2 * P * t + u : 2 * P * (t + 1) : 2] for t in (2 * pair, 2 * pair + 1) for u in range(2)]
+
+        def turn_surv(words, pair, turned, copy=nc.scalar.copy):
             bank = take("s_bank")
-            presorted = sorted_of.get((g, h, pair))
-            for s in range(2):
-                t = 2 * pair + s
-                for u in range(2):
-                    nc.tensor.transpose(
-                        bank[:, (2 * s + u) * P : (2 * s + u + 1) * P],
-                        words[:, 2 * P * t + u : 2 * P * (t + 1) : 2]
-                        if presorted is None
-                        else presorted[:, (2 * s + u) * P : (2 * s + u + 1) * P],
-                        ident[:],
-                    )
+            for n, some in enumerate(words):
+                nc.tensor.transpose(bank[:, n * P : (n + 1) * P], some, ident[:])
             copy(
-                out=grouped[:].bitcast(F32)[:, pair * PASS : (pair + 1) * PASS].rearrange(
+                out=turned[:].bitcast(F32)[:, pair * PASS : (pair + 1) * PASS].rearrange(
                     "p (s r u) -> p s r u", s=2, u=2
                 ),
                 in_=bank[:].rearrange("p (s u r) -> p s r u", s=2, u=2),
             )
 
-        def quantise_surv(g, h, grouped):
+        def quantise_surv(g, h, turned):
             nc.vector.quantize_mx(
                 out=surv_codes[HALVES * g + h][:].bitcast(FP8X4),
                 scales=surv_scales[HALVES * g + h][:],
-                in_=grouped[:],
+                in_=turned[:],
             )
 
-        def spread_leak(g, blocks):
-            for j0 in range(0, len(blocks), PACK):
-                bank = take("s_bank")
-                some = blocks[j0 : j0 + PACK]
-                for j, b in enumerate(some):
-                    m = BLOCKS * g + b
-                    nc.tensor.transpose(
-                        bank[:, j * P : (j + 1) * P], leak_neg[:, m : m + 1].to_broadcast([P, P]), ident[:]
-                    )
-                nc.scalar.copy(out=leak_spread[g][:, j0 * P : (j0 + len(some)) * P], in_=bank[:, : len(some) * P])
+        def spread_leak(g):
+            bank = take("s_bank")
+            for j, b in enumerate(direct_blocks[g]):
+                m = BLOCKS * g + b
+                nc.tensor.transpose(
+                    bank[:, j * P : (j + 1) * P], leak_neg[:, m : m + 1].to_broadcast([P, P]), ident[:]
+                )
+            width = len(direct_blocks[g]) * P
+            nc.scalar.copy(out=leak_spread[g][:, :width], in_=bank[:, :width])
 
         def w_block(g, b):
             return (
@@ -170,7 +157,7 @@ def tile_passive_radar_ambiguity_s14_kernel(
                 w_scales[:, g * L + P * b : g * L + P * (b + 1)],
             )
 
-        def steer_cells_first(g, b, h):
+        def steer_turned(g, b, h):
             words, scales = w_block(g, b)
             bank = take("s_bank")
             nc.tensor.matmul_mx(
@@ -182,7 +169,7 @@ def tile_passive_radar_ambiguity_s14_kernel(
                 start=True,
                 stop=True,
             )
-            clean = take("clean_ct")
+            clean = take("clean_turned")
             m = BLOCKS * g + b
             nc.scalar.activation(out=clean[:], in_=bank[:], func=ACT.Identity, bias=leak_neg[:, m : m + 1], scale=1.0)
             return clean
@@ -193,7 +180,7 @@ def tile_passive_radar_ambiguity_s14_kernel(
                 nc.tensor.transpose(bank[:, t * P : (t + 1) * P], clean[:, t * P : (t + 1) * P], ident[:])
             return bank
 
-        def steer_time_first(g, b, h):
+        def steer_direct(g, b, h):
             words, scales = w_block(g, b)
             bank = take("v_bank")
             for t in range(PACK):
@@ -208,116 +195,93 @@ def tile_passive_radar_ambiguity_s14_kernel(
                 )
             return bank
 
-        def ref_block(g, b, h):
-            side, c0 = divmod(b * P, ref_width[g])
-            return ref_rows[g, h][side][:].rearrange("p (t c) -> p t c", t=PACK)[:, :, c0 : c0 + P]
-
-        def subtract_leak(g, j, bank, interleave):
-            clean = take("clean_tc")
-            spread = leak_spread[g][:, j * P : (j + 1) * P]
-            if interleave:
-                nc.vector.tensor_tensor(
-                    out=clean[:].rearrange("p (c t) -> p c t", t=PACK),
-                    in0=bank[:].rearrange("p (t c) -> p c t", t=PACK),
-                    in1=spread.unsqueeze(2).to_broadcast([P, P, PACK]),
-                    op=ALU.add,
-                )
-            else:
-                nc.vector.tensor_tensor(
-                    out=clean[:].rearrange("p (t c) -> p t c", t=PACK),
-                    in0=bank[:].rearrange("p (t c) -> p t c", t=PACK),
-                    in1=spread.unsqueeze(1).to_broadcast([P, PACK, P]),
-                    op=ALU.add,
-                )
+        def subtract_leak(g, b, bank):
+            clean = take("clean_direct")
+            j = direct_blocks[g].index(b)
+            nc.vector.tensor_tensor(
+                out=clean[:].rearrange("p (t c) -> p t c", t=PACK),
+                in0=bank[:].rearrange("p (t c) -> p t c", t=PACK),
+                in1=leak_spread[g][:, j * P : (j + 1) * P].unsqueeze(1).to_broadcast([P, PACK, P]),
+                op=ALU.add,
+            )
             return clean
 
-        def mix(g, b, h, clean, mixed):
+        mixed_of, halves_mixed, finished = {}, {}, []
+
+        def mix(g, b, h, clean):
+            if (g, b) not in mixed_of:
+                mixed_of[g, b] = take("mixed")
+            part, c0 = divmod(b * P, ref_width[g])
+            ref_block = ref_rows[g, h][part][:].rearrange("p (t c) -> p t c", t=PACK)[:, :, c0 : c0 + P]
             nc.vector.tensor_tensor(
-                out=mixed[:, h * PASS : (h + 1) * PASS].rearrange("p (c i t) -> p c t i", i=RUN, t=PACK),
+                out=mixed_of[g, b][:, h * PASS : (h + 1) * PASS].rearrange("p (c i t) -> p c t i", i=RUN, t=PACK),
                 in0=clean[:].rearrange("p (t c i) -> p c t i", t=PACK, i=RUN),
-                in1=ref_block(g, b, h).rearrange("p t (c i) -> p c t i", i=RUN),
+                in1=ref_block.rearrange("p t (c i) -> p c t i", i=RUN),
                 op=ALU.mult,
             )
+            halves_mixed[g, b] = halves_mixed.get((g, b), 0) + 1
+            if halves_mixed[g, b] == HALVES:
+                finished.append((g, b))
 
-        def mix_gpsimd(g, b, h, clean, mixed):
-            nc.gpsimd.tensor_tensor(
-                out=mixed[:, h * PASS : (h + 1) * PASS].rearrange("p (c t) -> p c t", t=PACK),
-                in0=clean[:].rearrange("p (c t) -> p c t", t=PACK),
-                in1=ref_block(g, b, h).rearrange("p t c -> p c t"),
-                op=ALU.mult,
-            )
+        def quantise_mixed(blocks):
+            quantised = []
+            for g, b in blocks:
+                finished.remove((g, b))
+                codes, scales = take("mixed_codes"), take("mixed_scales")
+                nc.vector.quantize_mx(out=codes[:].bitcast(FP8X4), scales=scales[:], in_=mixed_of[g, b][:])
+                quantised.append((g, b, codes, scales))
+            return quantised
 
-        def quantise_mixed(mixed):
-            codes, scales = take("mixed_codes"), take("mixed_scales")
-            nc.vector.quantize_mx(out=codes[:].bitcast(FP8X4), scales=scales[:], in_=mixed[:])
-            return codes, scales
-
-        def doppler(g, b, codes, scales, copy=nc.scalar.copy):
-            bank = take("s_bank")
-            for h in range(HALVES):
-                nc.tensor.matmul_mx(
-                    out=bank[:],
-                    lhsT=codes[:, h * P : (h + 1) * P].bitcast(FP8X4),
-                    lhsT_scale=scales[:, h * P : (h + 1) * P],
-                    rhs=d_words[g][:, h * 2 * F : (h + 1) * 2 * F].bitcast(FP4X4),
-                    rhs_scale=d_scales[:, (HALVES * g + h) * F : (HALVES * g + h + 1) * F],
-                    start=(h == 0),
-                    stop=(h == HALVES - 1),
-                )
-            result = take("result")
-            copy(out=result[:], in_=bank[:])
-            nc.sync.dma_start(out=out[g, b * P : (b + 1) * P, :], in_=result[:])
+        def doppler(quantised, copy=nc.scalar.copy):
+            for g, b, codes, scales in quantised:
+                bank = take("s_bank")
+                for h in range(HALVES):
+                    nc.tensor.matmul_mx(
+                        out=bank[:],
+                        lhsT=codes[:, h * P : (h + 1) * P].bitcast(FP8X4),
+                        lhsT_scale=scales[:, h * P : (h + 1) * P],
+                        rhs=d_words[g][:, h * 2 * F : (h + 1) * 2 * F].bitcast(FP4X4),
+                        rhs_scale=d_scales[:, (HALVES * g + h) * F : (HALVES * g + h + 1) * F],
+                        start=(h == 0),
+                        stop=(h == HALVES - 1),
+                    )
+                result = take("result")
+                copy(out=result[:], in_=bank[:])
+                nc.sync.dma_start(out=out[g, b * P : (b + 1) * P, :], in_=result[:])
 
         plan, direct_blocks = [], []
         for g in range(G):
-            first_block, direct_all = 0, []
-            for r, (n_turned, n_direct) in enumerate(SETS[g]):
-                blocks = list(range(first_block, first_block + n_turned + n_direct))
-                first_block += len(blocks)
-                tu = [(b, h) for b in blocks[n_direct:] for h in range(HALVES)]
-                du = [(len(direct_all) + j, b, h) for j, b in enumerate(blocks[:n_direct]) for h in range(HALVES)]
-                for h in range(HALVES):
-                    if r > 0:
-                        plan.append((g, HALVES * r + h, tu[h * n_turned : (h + 1) * n_turned], du[h * n_direct : (h + 1) * n_direct]))
+            direct_blocks.append([])
+            for quad, n_direct in enumerate(DIRECT_IN_QUAD[g % 2]):
+                blocks = list(range(QUAD * quad, QUAD * (quad + 1)))
+                direct_blocks[g].extend(blocks[:n_direct])
+                ways = [[(b, h) for b in some for h in range(HALVES)] for some in (blocks[n_direct:], blocks[:n_direct])]
+                for s in range(HALVES):
+                    if quad == 0:
+                        turned, direct = [units[s::HALVES] for units in ways]
                     else:
-                        plan.append((g, HALVES * r + h, tu[h::HALVES], du[h::HALVES]))
-                direct_all.extend(blocks[:n_direct])
-            direct_blocks.append(direct_all)
+                        turned, direct = [units[s * len(units) // HALVES : (s + 1) * len(units) // HALVES] for units in ways]
+                    plan.append((g, HALVES * quad + s, turned, direct))
 
         make_identity(nc, ident[:])
         nc.vector.memset(w_scales[:].bitcast(I32), 0)
-        nc.gpsimd.memset(warm[:], 0.0)
-        nc.scalar.activation(out=warm[:], in_=warm[:], func=ACT.Identity, bias=0.0, scale=1.0)
+        nc.scalar.activation(out=leak_neg_rows[:], in_=ident[:], func=ACT.Identity, bias=0.0, scale=0.0)
         nc.sync.dma_start(out=leak_rows[:], in_=leak.rearrange("g (b p) -> (g b) p", p=P))
-        for pair in range(2):
-            nc.sync.dma_start(
-                out=surv_rows[0][:, pair * 2 * K : (pair + 1) * 2 * K].rearrange("p (t k) -> p t k", t=2),
-                in_=surv[0, :PASS, :].rearrange("(p t) k -> p t k", t=PACK)[:, 2 * pair : 2 * pair + 2, :],
-            )
+        for pair in range(PAIRS):
+            load_surv(0, 0, slice(2 * pair, 2 * pair + 2))
         load_surv(0, 1)
         load_scales(w_scales, steer_scales)
         load_w(0)
-        nc.vector.memset(leak_neg_rows[:], 0.0)
         nc.vector.memset(d_scales[:].bitcast(I32), 0)
-        for what in "rRab01d":
-            if what == "r":
-                load_ref(0, 0, 0)
-            if what == "s":
-                load_surv(0, 1)
-            if what == "R":
-                load_ref(0, 1, 0)
-            if what == "a":
-                load_surv(1, 0)
-            if what == "b":
-                load_surv(1, 1)
-            if what == "d":
-                load_scales(d_scales, doppler_scales)
-                load_d(0)
-            if what == "0":
-                load_ref(0, 0, 1)
-            if what == "1":
-                load_ref(0, 1, 1)
-        def load_group(g):
+        for h in range(HALVES):
+            load_ref(0, h, 0)
+        for h in range(HALVES):
+            load_surv(1, h)
+        for h in range(HALVES):
+            load_ref(0, h, 1)
+        load_scales(d_scales, doppler_scales)
+        load_d(0)
+        for g in range(1, G):
             load_w(g)
             for h in range(HALVES):
                 load_ref(g, h, 0)
@@ -326,144 +290,75 @@ def tile_passive_radar_ambiguity_s14_kernel(
                 for h in range(HALVES):
                     load_surv(g + 1, h)
 
-        load_at = [0,-1,-1,-1]
-        for g in range(1, G):
-            if load_at[g] < 0:
-                load_group(g)
-
         nc.vector.tensor_scalar(
             out=leak_neg_rows[: G * BLOCKS, :], in0=leak_rows[:], scalar1=-1.0, scalar2=None, op0=ALU.mult
         )
-        first = [take("grouped"), take("grouped")]
-        if 1:
-            sort_words(0, 0, 0, nc.vector.tensor_copy)
-            sort_words(0, 0, 1, nc.vector.tensor_copy)
+        first_half, second_half = take("surv_turned"), take("surv_turned")
+        first_words = [sort_words(0, 0, pair) for pair in range(PAIRS)]
         bank = take("s_bank")
         nc.tensor.transpose(bank[:, :P], leak_neg_rows[:], ident[:])
         nc.scalar.copy(out=leak_neg[:], in_=bank[:, : G * BLOCKS])
-        turn_surv(0, 0, 0, first[0], nc.scalar.copy)
-        if 1:
-            sort_words(0, 1, 0, nc.vector.tensor_copy)
-            sort_words(0, 1, 1, nc.vector.tensor_copy)
-        turn_surv(0, 0, 1, first[0], nc.vector.tensor_copy)
-        spread_leak(0, direct_blocks[0])
-        quantise_surv(0, 0, first[0])
-        turn_surv(0, 1, 0, first[1], nc.scalar.copy)
-        turn_surv(0, 1, 1, first[1], nc.scalar.copy)
+        turn_surv(first_words[0], 0, first_half)
+        second_words = [sort_words(0, 1, pair) for pair in range(PAIRS)]
+        turn_surv(first_words[1], 1, first_half, nc.vector.tensor_copy)
+        spread_leak(0)
+        quantise_surv(0, 0, first_half)
+        for pair in range(PAIRS):
+            turn_surv(second_words[pair], pair, second_half)
 
-        to_quantise, to_multiply, to_mix, surv_ready = [], [], [], [(0, 1, first[1])]
-        mixed_of, halves_done = {}, {}
-        direct_count = 0
-        surv_next = []
-
-        def mix_unit(how, g, b, h, clean):
-            if (g, b) not in mixed_of:
-                mixed_of[g, b] = take("mixed")
-            how(g, b, h, clean, mixed_of[g, b])
-            halves_done[g, b] = halves_done.get((g, b), 0) + 1
-            if halves_done[g, b] == HALVES:
-                to_quantise.append((g, b))
-
-        to_multiply = [[] for lag in range(LAG)]
-        pending = []
-        for n, (g, i, turned, direct) in enumerate(plan):
-            count = HALVES * len(SETS[g])
-            share = -(-BLOCKS // count) if n < len(plan) - 1 else BLOCKS
-            ready = to_quantise[:share]
-            to_quantise[:share] = []
-            quantised = []
-            for g_load in range(1, G):
-                if load_at[g_load] == n:
-                    load_group(g_load)
-            for what in ("xAySYmTUOC" if n == 0 else "OASTqumoQuQouQo" if n == len(plan) - 1 else "xOYASTUqmC" if n == len(plan) - 2 else ORDER):
-                if what == "y":
-                    cleans = [steer_cells_first(g, b, h) for b, h in turned]
-                if what == "p":
-                    sort_words(0, 1, 0)
-                    sort_words(0, 1, 1)
-                if what == "P":
-                    turn_surv(0, 1, 0, first[1], nc.scalar.copy)
-                    turn_surv(0, 1, 1, first[1], nc.scalar.copy)
-                    surv_ready.append((0, 1, first[1]))
-                if what == "A":
-                    todo = [(unit, steer_time_first(g, unit[1], unit[2])) for unit in direct]
-                if what == "O":
-                    for args in to_multiply.pop(0):
-                        doppler(*args)
-                if what == "Y" and n + 1 < len(plan):
-                    cleans_next = [steer_cells_first(plan[n + 1][0], b, h) for b, h in plan[n + 1][2]]
-                if what == "T":
-                    to_mix.extend([(g, b, h, turn_clean(clean)) for (b, h), clean in zip(turned, cleans)])
-                if what == "C" and g + 1 < G:
-                    for c in range(2 * HALVES):
-                        if min(c, count - 2) == i:
-                            h, pair = divmod(c, 2)
-                            if pair == 0:
-                                grouped = take("grouped")
-                            turn_surv(g + 1, h, pair, grouped, nc.scalar.copy)
-                            if pair == 1:
-                                surv_next.append((g + 1, h, grouped))
-                    if i == count - 1:
-                        spread_leak(g + 1, direct_blocks[g + 1])
-                if what == "D" and g + 1 < G:
-                    for c in range(2 * HALVES):
-                        if (min(c, count - 2) == i + 1 and (g or i + 1 > min([min(c, count - 2) for c in range(4)]))) or (g == 0 and i == min(c, count - 2) == (min(c, count - 2) if c == 0 else i) and i == min([min(c, count - 2) for c in range(4)])):
-                            sort_words(g + 1, *divmod(c, 2))
-                        if i == count - 1 and g + 2 < G and c == 0:
-                            sort_words(g + 2, *divmod(c, 2))
-                if what == "u" and to_mix:
-                    mix_unit(mix, *to_mix.pop(0))
-                if what == "U":
-                    for args in to_mix:
-                        mix_unit(mix, *args)
-                    to_mix = []
-                if what in "sS":
-                    for (j, b, h), bank in todo[:1] if what == "s" else todo:
-                        direct_count += 1
-                        first_here = (j, b, h) == direct[0]
-                        on = False
-                        clean = subtract_leak(g, j, bank, on)
-                        if on:
-                            mix_unit(mix_gpsimd, g, b, h, clean)
-                        else:
-                            pending.append((g, b, h, clean))
-                    todo = todo[1:] if what == "s" else []
-                if what == "q":
-                    for gq, b in ready:
-                        quantised.append((gq, b) + quantise_mixed(mixed_of[gq, b]))
-                    ready = []
-                if what == "Q":
-                    for gq, b in ready + to_quantise:
-                        quantised.append((gq, b) + quantise_mixed(mixed_of[gq, b]))
-                    to_quantise.clear()
-                    ready = []
-                if what == "o":
-                    for some in to_multiply:
-                        for args in some:
-                            doppler(*args)
-                        some.clear()
-                    for args in quantised:
-                        doppler(*args, copy=nc.vector.tensor_copy if len(halves_done) == G * BLOCKS and all([v == 2 for v in halves_done.values()]) and args is quantised[-1] and not to_quantise else nc.scalar.copy)
-                    quantised = []
-                if what == "m":
-                    for args in pending:
-                        mix_unit(mix, *args)
-                    pending = []
-                if what == "x":
-                    for args in surv_ready:
-                        quantise_surv(*args)
-                    surv_ready = []
-            to_multiply.append(quantised)
+        surv_to_quantise = [(0, 1, second_half)]
+        waiting = [[] for lag in range(DOPPLER_LAG)]
+        for n, (g, step, turned, direct) in enumerate(plan[:-1]):
+            g_next, step_next, turned_next, direct_next = plan[n + 1]
+            to_quantise = finished[:BLOCKS_PER_STEP]
+            for args in surv_to_quantise:
+                quantise_surv(*args)
+            surv_to_quantise = []
+            doppler(waiting.pop(0))
+            if n == 0:
+                banks = [steer_direct(g, b, h) for b, h in direct]
+                cleans = [steer_turned(g, b, h) for b, h in turned]
+                subtracted = [subtract_leak(g, b, bank) for (b, h), bank in zip(direct, banks)]
+                cleans_next = [steer_turned(g_next, b, h) for b, h in turned_next]
+                for (b, h), clean in zip(direct, subtracted):
+                    mix(g, b, h, clean)
+                subtracted = []
+            else:
+                cleans_next = [steer_turned(g_next, b, h) for b, h in turned_next]
+                banks = [steer_direct(g, b, h) for b, h in direct]
+                subtracted = [subtract_leak(g, b, bank) for (b, h), bank in zip(direct, banks)]
+            banks = [turn_clean(clean) for clean in cleans]
+            for (b, h), bank in zip(turned, banks):
+                mix(g, b, h, bank)
+            waiting.append(quantise_mixed(to_quantise))
+            for (b, h), clean in zip(direct, subtracted):
+                mix(g, b, h, clean)
             cleans = cleans_next
-            surv_ready, surv_next = surv_ready + surv_next, []
 
-        for args in pending:
-            mix_unit(mix, *args)
-        for args in to_mix:
-            mix_unit(mix, *args)
-        for some in to_multiply:
-            for args in some:
-                doppler(*args)
-        for k, (gq, b) in enumerate(to_quantise):
-            last = k == len(to_quantise) - 1
-            doppler(gq, b, *quantise_mixed(mixed_of[gq, b]), copy=nc.vector.tensor_copy if last else nc.scalar.copy)
+            if g + 1 < G:
+                for chunk in range(HALVES * PAIRS):
+                    if min(chunk, STEPS - 2) == step:
+                        h, pair = divmod(chunk, PAIRS)
+                        if pair == 0:
+                            next_half = take("surv_turned")
+                        turn_surv(stepped_words(g + 1, h, pair), pair, next_half)
+                        if pair == PAIRS - 1:
+                            surv_to_quantise.append((g + 1, h, next_half))
+                if step == STEPS - 1:
+                    spread_leak(g + 1)
+
+        g, step, turned, direct = plan[-1]
+        doppler(waiting.pop(0))
+        banks = [steer_direct(g, b, h) for b, h in direct]
+        subtracted = [subtract_leak(g, b, bank) for (b, h), bank in zip(direct, banks)]
+        banks = [turn_clean(clean) for clean in cleans]
+        quantised = quantise_mixed(list(finished))
+        mix(g, *turned[0], banks[0])
+        for (b, h), clean in zip(direct, subtracted):
+            mix(g, b, h, clean)
+        doppler(waiting.pop(0) + quantised)
+        quantised = quantise_mixed(list(finished))
+        mix(g, *turned[1], banks[1])
+        doppler(quantised)
+        mix(g, *turned[2], banks[2])
+        doppler(quantise_mixed(list(finished)), nc.vector.tensor_copy)

from contextlib import ExitStack

import concourse.mybir as mybir
from concourse.masks import make_identity

G, T, K, L, F = 4, 1024, 512, 1024, 512
FLOPS = 2 * G * T * K * L + 2 * G * L * T * F

F32 = mybir.dt.float32
BF16 = mybir.dt.bfloat16
I32 = mybir.dt.int32
U32 = mybir.dt.uint32
U8 = mybir.dt.uint8
FP8X4 = mybir.dt.float8_e4m3fn_x4
FP4X4 = mybir.dt.float4_e2m1fn_x4
ALU = mybir.AluOpType
ACT = mybir.ActivationFunctionType

P = 128
PACK = 4
PASS = P * PACK
HALVES = T // PASS
BLOCKS = L // P
QUAD = 4
STEPS = HALVES * BLOCKS // QUAD
PAIRS = 2

DIRECT_IN_QUAD = ((2, 1), (1, 1))
RUN = 2
DOPPLER_LAG = 2
BLOCKS_PER_STEP = BLOCKS // STEPS


def tile_passive_radar_ambiguity_s14_kernel(
    tc, surv, ref, leak, steer_words, steer_scales, doppler_words, doppler_scales, out
):
    nc = tc.nc
    with ExitStack() as ctx:
        sb = ctx.enter_context(tc.tile_pool(name="sb", bufs=1))
        ps = ctx.enter_context(tc.psum_pool(name="ps", bufs=1))
        ctx.enter_context(tc.manual_schedule())

        def tiles(name, count, shape, dtype):
            return [sb.tile(shape, dtype, name="%s%d" % (name, i), align_bytes=64) for i in range(count)]

        rings = {
            "s_bank": [ps.tile([P, PASS], F32, name="s_bank%d" % i) for i in range(4)],
            "v_bank": [ps.tile([P, PASS], F32, name="v_bank%d" % i) for i in range(4)],
            "clean_turned": tiles("clean_turned", 6, [P, PASS], F32),
            "clean_direct": tiles("clean_direct", 3, [P, PASS], F32),
            "sorted_words": tiles("sorted_words", 3, [P, PASS], F32),
            "surv_turned": tiles("surv_turned", 2, [P, PASS * PACK], BF16),
            "mixed": tiles("mixed", 2 * QUAD, [P, HALVES * PASS], BF16),
            "mixed_codes": tiles("mixed_codes", 2 * QUAD, [P, HALVES * P], U32),
            "mixed_scales": tiles("mixed_scales", 2 * QUAD, [P, HALVES * P], U8),
            "result": tiles("result", 12, [P, F], F32),
        }
        taken = {name: 0 for name in rings}

        def take(name):
            tile = rings[name][taken[name] % len(rings[name])]
            taken[name] += 1
            return tile

        ident = sb.tile([P, P], F32, name="ident")
        w_scales = sb.tile([P, G * L], U8, name="w_scales", align_bytes=64)
        d_scales = sb.tile([P, G * HALVES * F], U8, name="d_scales", align_bytes=64)
        w_words = tiles("w_words", G, [P, 2 * L], U8)
        d_words = tiles("d_words", G, [P, HALVES * 2 * F], U8)
        surv_rows = tiles("surv_rows", G * HALVES, [P, PACK * K], BF16)
        surv_codes = tiles("surv_codes", G * HALVES, [P, PASS], U32)
        surv_scales = tiles("surv_scales", G * HALVES, [P, PASS], U8)
        ref_width = [QUAD * P] + [L] * (G - 1)
        ref_rows = {
            (g, h): tiles("ref_rows%d_%d_" % (g, h), L // ref_width[g], [P, PACK * ref_width[g]], BF16)
            for g in range(G)
            for h in range(HALVES)
        }
        leak_rows = sb.tile([G * BLOCKS, P], BF16, name="leak_rows")
        leak_neg_rows = sb.tile([P, P], F32, name="leak_neg_rows")
        leak_neg = sb.tile([P, G * BLOCKS], F32, name="leak_neg")
        leak_spread = tiles("leak_spread", G, [P, QUAD * P], F32)

        def load_surv(g, h, slots=slice(0, PACK)):
            nc.sync.dma_start(
                out=surv_rows[HALVES * g + h][:, slots.start * K : slots.stop * K].rearrange("p (t k) -> p t k", k=K),
                in_=surv[g, h * PASS : (h + 1) * PASS, :].rearrange("(p t) k -> p t k", t=PACK)[:, slots, :],
            )

        def load_ref(g, h, part):
            cells = slice(part * ref_width[g], (part + 1) * ref_width[g])
            nc.sync.dma_start(
                out=ref_rows[g, h][part][:].rearrange("p (t c) -> p t c", t=PACK),
                in_=ref[g, h * PASS : (h + 1) * PASS, cells].rearrange("(p t) c -> p t c", t=PACK),
            )

        def load_w(g):
            nc.sync.dma_start(out=w_words[g][:].bitcast(I32), in_=steer_words[g].bitcast(I32))

        def load_d(g):
            nc.sync.dma_start(
                out=d_words[g][:].bitcast(I32).rearrange("p (h n) -> p h n", h=HALVES),
                in_=doppler_words[HALVES * g : HALVES * (g + 1)].bitcast(I32).rearrange("h p n -> p h n"),
            )

        def load_scales(scales, rows):
            for q in range(4):
                nc.sync.dma_start(
                    out=scales[32 * q : 32 * q + 4, :].bitcast(I32).rearrange("r (g n) -> r g n", g=rows.shape[0]),
                    in_=rows[:, 4 * q : 4 * q + 4, :].bitcast(I32).rearrange("g r n -> r g n"),
                )

        def sort_words(g, h, pair):
            tile = take("sorted_words")
            words = surv_rows[HALVES * g + h][:].bitcast(F32)[:, pair * PASS : (pair + 1) * PASS]
            nc.vector.tensor_copy(
                out=tile[:].rearrange("p (s u r) -> p s u r", s=2, u=2),
                in_=words.rearrange("p (s r u) -> p s u r", s=2, u=2),
            )
            return [tile[:, n * P : (n + 1) * P] for n in range(4)]

        def stepped_words(g, h, pair):
            words = surv_rows[HALVES * g + h][:].bitcast(F32)
            return [words[:, 2 * P * t + u : 2 * P * (t + 1) : 2] for t in (2 * pair, 2 * pair + 1) for u in range(2)]

        def turn_surv(words, pair, turned, copy=nc.scalar.copy):
            bank = take("s_bank")
            for n, some in enumerate(words):
                nc.tensor.transpose(bank[:, n * P : (n + 1) * P], some, ident[:])
            copy(
                out=turned[:].bitcast(F32)[:, pair * PASS : (pair + 1) * PASS].rearrange(
                    "p (s r u) -> p s r u", s=2, u=2
                ),
                in_=bank[:].rearrange("p (s u r) -> p s r u", s=2, u=2),
            )

        def quantise_surv(g, h, turned):
            nc.vector.quantize_mx(
                out=surv_codes[HALVES * g + h][:].bitcast(FP8X4),
                scales=surv_scales[HALVES * g + h][:],
                in_=turned[:],
            )

        def spread_leak(g):
            bank = take("s_bank")
            for j, b in enumerate(direct_blocks[g]):
                m = BLOCKS * g + b
                nc.tensor.transpose(
                    bank[:, j * P : (j + 1) * P], leak_neg[:, m : m + 1].to_broadcast([P, P]), ident[:]
                )
            width = len(direct_blocks[g]) * P
            nc.scalar.copy(out=leak_spread[g][:, :width], in_=bank[:, :width])

        def w_block(g, b):
            return (
                w_words[g][:, 2 * P * b : 2 * P * (b + 1)].bitcast(FP4X4),
                w_scales[:, g * L + P * b : g * L + P * (b + 1)],
            )

        def steer_turned(g, b, h):
            words, scales = w_block(g, b)
            bank = take("s_bank")
            nc.tensor.matmul_mx(
                out=bank[:],
                lhsT=words,
                lhsT_scale=scales,
                rhs=surv_codes[HALVES * g + h][:].bitcast(FP8X4),
                rhs_scale=surv_scales[HALVES * g + h][:],
                start=True,
                stop=True,
            )
            clean = take("clean_turned")
            m = BLOCKS * g + b
            nc.scalar.activation(out=clean[:], in_=bank[:], func=ACT.Identity, bias=leak_neg[:, m : m + 1], scale=1.0)
            return clean

        def turn_clean(clean):
            bank = take("v_bank")
            for t in range(PACK):
                nc.tensor.transpose(bank[:, t * P : (t + 1) * P], clean[:, t * P : (t + 1) * P], ident[:])
            return bank

        def steer_direct(g, b, h):
            words, scales = w_block(g, b)
            bank = take("v_bank")
            for t in range(PACK):
                nc.tensor.matmul_mx(
                    out=bank[:, t * P : (t + 1) * P],
                    lhsT=surv_codes[HALVES * g + h][:, t * P : (t + 1) * P].bitcast(FP8X4),
                    lhsT_scale=surv_scales[HALVES * g + h][:, t * P : (t + 1) * P],
                    rhs=words,
                    rhs_scale=scales,
                    start=True,
                    stop=True,
                )
            return bank

        def subtract_leak(g, b, bank):
            clean = take("clean_direct")
            j = direct_blocks[g].index(b)
            nc.vector.tensor_tensor(
                out=clean[:].rearrange("p (t c) -> p t c", t=PACK),
                in0=bank[:].rearrange("p (t c) -> p t c", t=PACK),
                in1=leak_spread[g][:, j * P : (j + 1) * P].unsqueeze(1).to_broadcast([P, PACK, P]),
                op=ALU.add,
            )
            return clean

        mixed_of, halves_mixed, finished = {}, {}, []

        def mix(g, b, h, clean):
            if (g, b) not in mixed_of:
                mixed_of[g, b] = take("mixed")
            part, c0 = divmod(b * P, ref_width[g])
            ref_block = ref_rows[g, h][part][:].rearrange("p (t c) -> p t c", t=PACK)[:, :, c0 : c0 + P]
            nc.vector.tensor_tensor(
                out=mixed_of[g, b][:, h * PASS : (h + 1) * PASS].rearrange("p (c i t) -> p c t i", i=RUN, t=PACK),
                in0=clean[:].rearrange("p (t c i) -> p c t i", t=PACK, i=RUN),
                in1=ref_block.rearrange("p t (c i) -> p c t i", i=RUN),
                op=ALU.mult,
            )
            halves_mixed[g, b] = halves_mixed.get((g, b), 0) + 1
            if halves_mixed[g, b] == HALVES:
                finished.append((g, b))

        def quantise_mixed(blocks):
            quantised = []
            for g, b in blocks:
                finished.remove((g, b))
                codes, scales = take("mixed_codes"), take("mixed_scales")
                nc.vector.quantize_mx(out=codes[:].bitcast(FP8X4), scales=scales[:], in_=mixed_of[g, b][:])
                quantised.append((g, b, codes, scales))
            return quantised

        def doppler(quantised, copy=nc.scalar.copy):
            for g, b, codes, scales in quantised:
                bank = take("s_bank")
                for h in range(HALVES):
                    nc.tensor.matmul_mx(
                        out=bank[:],
                        lhsT=codes[:, h * P : (h + 1) * P].bitcast(FP8X4),
                        lhsT_scale=scales[:, h * P : (h + 1) * P],
                        rhs=d_words[g][:, h * 2 * F : (h + 1) * 2 * F].bitcast(FP4X4),
                        rhs_scale=d_scales[:, (HALVES * g + h) * F : (HALVES * g + h + 1) * F],
                        start=(h == 0),
                        stop=(h == HALVES - 1),
                    )
                result = take("result")
                copy(out=result[:], in_=bank[:])
                nc.sync.dma_start(out=out[g, b * P : (b + 1) * P, :], in_=result[:])

        plan, direct_blocks = [], []
        for g in range(G):
            direct_blocks.append([])
            for quad, n_direct in enumerate(DIRECT_IN_QUAD[g % 2]):
                blocks = list(range(QUAD * quad, QUAD * (quad + 1)))
                direct_blocks[g].extend(blocks[:n_direct])
                ways = [[(b, h) for b in some for h in range(HALVES)] for some in (blocks[n_direct:], blocks[:n_direct])]
                for s in range(HALVES):
                    if quad == 0:
                        turned, direct = [units[s::HALVES] for units in ways]
                    else:
                        turned, direct = [units[s * len(units) // HALVES : (s + 1) * len(units) // HALVES] for units in ways]
                    plan.append((g, HALVES * quad + s, turned, direct))

        make_identity(nc, ident[:])
        nc.vector.memset(w_scales[:].bitcast(I32), 0)
        nc.scalar.activation(out=leak_neg_rows[:], in_=ident[:], func=ACT.Identity, bias=0.0, scale=0.0)
        nc.sync.dma_start(out=leak_rows[:], in_=leak.rearrange("g (b p) -> (g b) p", p=P))
        for pair in range(PAIRS):
            load_surv(0, 0, slice(2 * pair, 2 * pair + 2))
        load_surv(0, 1)
        load_scales(w_scales, steer_scales)
        load_w(0)
        nc.vector.memset(d_scales[:].bitcast(I32), 0)
        for h in range(HALVES):
            load_ref(0, h, 0)
        for h in range(HALVES):
            load_surv(1, h)
        for h in range(HALVES):
            load_ref(0, h, 1)
        load_scales(d_scales, doppler_scales)
        load_d(0)
        for g in range(1, G):
            load_w(g)
            for h in range(HALVES):
                load_ref(g, h, 0)
            load_d(g)
            if g + 1 < G:
                for h in range(HALVES):
                    load_surv(g + 1, h)

        nc.vector.tensor_scalar(
            out=leak_neg_rows[: G * BLOCKS, :], in0=leak_rows[:], scalar1=-1.0, scalar2=None, op0=ALU.mult
        )
        first_half, second_half = take("surv_turned"), take("surv_turned")
        first_words = [sort_words(0, 0, pair) for pair in range(PAIRS)]
        bank = take("s_bank")
        nc.tensor.transpose(bank[:, :P], leak_neg_rows[:], ident[:])
        nc.scalar.copy(out=leak_neg[:], in_=bank[:, : G * BLOCKS])
        turn_surv(first_words[0], 0, first_half)
        second_words = [sort_words(0, 1, pair) for pair in range(PAIRS)]
        turn_surv(first_words[1], 1, first_half, nc.vector.tensor_copy)
        spread_leak(0)
        quantise_surv(0, 0, first_half)
        for pair in range(PAIRS):
            turn_surv(second_words[pair], pair, second_half)

        surv_to_quantise = [(0, 1, second_half)]
        waiting = [[] for lag in range(DOPPLER_LAG)]
        for n, (g, step, turned, direct) in enumerate(plan[:-1]):
            g_next, step_next, turned_next, direct_next = plan[n + 1]
            to_quantise = finished[:BLOCKS_PER_STEP]
            for args in surv_to_quantise:
                quantise_surv(*args)
            surv_to_quantise = []
            doppler(waiting.pop(0))
            if n == 0:
                banks = [steer_direct(g, b, h) for b, h in direct]
                cleans = [steer_turned(g, b, h) for b, h in turned]
                subtracted = [subtract_leak(g, b, bank) for (b, h), bank in zip(direct, banks)]
                cleans_next = [steer_turned(g_next, b, h) for b, h in turned_next]
                for (b, h), clean in zip(direct, subtracted):
                    mix(g, b, h, clean)
                subtracted = []
            else:
                cleans_next = [steer_turned(g_next, b, h) for b, h in turned_next]
                banks = [steer_direct(g, b, h) for b, h in direct]
                subtracted = [subtract_leak(g, b, bank) for (b, h), bank in zip(direct, banks)]
            banks = [turn_clean(clean) for clean in cleans]
            for (b, h), bank in zip(turned, banks):
                mix(g, b, h, bank)
            waiting.append(quantise_mixed(to_quantise))
            for (b, h), clean in zip(direct, subtracted):
                mix(g, b, h, clean)
            cleans = cleans_next

            if g + 1 < G:
                for chunk in range(HALVES * PAIRS):
                    if min(chunk, STEPS - 2) == step:
                        h, pair = divmod(chunk, PAIRS)
                        if pair == 0:
                            next_half = take("surv_turned")
                        turn_surv(stepped_words(g + 1, h, pair), pair, next_half)
                        if pair == PAIRS - 1:
                            surv_to_quantise.append((g + 1, h, next_half))
                if step == STEPS - 1:
                    spread_leak(g + 1)

        g, step, turned, direct = plan[-1]
        doppler(waiting.pop(0))
        banks = [steer_direct(g, b, h) for b, h in direct]
        subtracted = [subtract_leak(g, b, bank) for (b, h), bank in zip(direct, banks)]
        banks = [turn_clean(clean) for clean in cleans]
        quantised = quantise_mixed(list(finished))
        mix(g, *turned[0], banks[0])
        for (b, h), clean in zip(direct, subtracted):
            mix(g, b, h, clean)
        doppler(waiting.pop(0) + quantised)
        quantised = quantise_mixed(list(finished))
        mix(g, *turned[1], banks[1])
        doppler(quantised)
        mix(g, *turned[2], banks[2])
        doppler(quantise_mixed(list(finished)), nc.vector.tensor_copy)
